import numpy as np
import ml_dtypes


def mxq(x, axis, fmt="e4m3"):
    dtype, down = {"e4m3": (ml_dtypes.float8_e4m3fn, 7), "e5m2": (ml_dtypes.float8_e5m2, 14)}[fmt]
    v = np.moveaxis(np.asarray(x, np.float32).astype(ml_dtypes.bfloat16).astype(np.float64), axis, -1)
    blocks = v.reshape(v.shape[:-1] + (-1, 32))
    amax = np.abs(blocks).max(-1, keepdims=True)
    byte = np.maximum(np.where(amax > 0, np.frexp(amax)[1] - 1 + 127, 0) - down, 1)
    scale = np.exp2(byte - 127.0)
    codes = (blocks / scale).astype(np.float32).astype(dtype).astype(np.float64)
    return np.moveaxis((codes * scale).reshape(v.shape), -1, axis)


WIDE = False


def mx_kscale(k):
    if not WIDE:
        return np.ones(k)
    levels = np.array([10, -10, 5, -5, 0])
    if k % 512:
        return np.exp2(np.random.permutation(np.resize(levels, k // 32))).repeat(32)
    a = np.empty((k // 512, 16))
    for p in range(k // 512):
        a[p, :8] = np.random.permutation(np.resize(levels, 8))
        for g in range(8):
            far = levels[np.abs(levels - a[p, g]) >= 10]
            a[p, g + 8] = far[np.random.randint(len(far))]
    return np.exp2(a.ravel()).repeat(32)


def f64(x):
    return np.asarray(x).astype(np.float64)


def striped(idx):
    return np.tile(idx.reshape(-1, 16).T, (8, 1)).astype(np.uint16)


def unstriped(offs):
    return offs[:16].T.reshape(-1).astype(np.int64)


def striped8(idx):
    return np.concatenate([x.reshape(-1, 16).T for x in idx]).astype(np.uint16)


def runs(offs, k):
    lists = np.stack([offs[16 * r : 16 * r + 16].T.reshape(-1) for r in range(8)]).astype(np.int64)
    return lists[np.arange(k) % 512 // 64]


def pack_weight(w):
    k, n = w.shape
    w = f64(np.asarray(w, np.float32).astype(ml_dtypes.bfloat16)).reshape(k // 32, 32, n)
    amax = np.abs(w).max(1)
    byte = np.clip(np.where(amax > 0, np.frexp(amax)[1] - 1 + 127 - 7, 1), 1, 254)
    scaled = (w * np.exp2(127.0 - byte)[:, None, :]).reshape(k, n).astype(np.float32)
    words = np.ascontiguousarray(scaled.reshape(k // 512, 128, 4, n).transpose(0, 1, 3, 2)).astype(ml_dtypes.float8_e4m3fn).view(np.uint8)
    return words, np.ascontiguousarray(byte.astype(np.uint8).reshape(k // 512, 16, n))


def unpack_weight(words, scales):
    g, p, n, _ = words.shape
    vals = np.ascontiguousarray(words).view(ml_dtypes.float8_e4m3fn).astype(np.float64) * np.repeat(np.exp2(scales.astype(np.float64) - 127.0), 8, axis=1)[..., None]
    return vals.transpose(0, 1, 3, 2).reshape(g * 512, n)


def sigmoid(v):
    return 1.0 / (1.0 + np.exp(-np.maximum(v, -700.0)))

def planes(y):
    n, m = y.shape
    v = y.astype(np.float32).astype(ml_dtypes.bfloat16).astype(np.float64).reshape(n // 32, 32, m)
    top = np.abs(v).max(1)
    byte = np.clip(np.where(top > 0, np.frexp(top)[1] - 1 + 127 - 7, 1), 1, 254)
    codes = (v * np.exp2(127.0 - byte)[:, None, :]).reshape(n, m).astype(np.float32).astype(ml_dtypes.float8_e4m3fn).view(np.uint8)
    words = codes.reshape(n // 512, 128, 4, m).transpose(0, 1, 3, 2)
    return np.ascontiguousarray(words), np.ascontiguousarray(byte.astype(np.uint8).reshape(n // 512, 16, m))


K, T, S, N = 1024, 2048, 512, 512


def setup_inputs():
    n = np.random.standard_normal
    s = mx_kscale(K)[:, None]
    packed_xT = pack_weight(n((K, T)) * s)
    return {
        "x_words": packed_xT[0],
        "x_scales": packed_xT[1],
        "cell": n((N, S)).astype(np.float32),
        "w1": (n((K, N)) / np.sqrt(K) / s).astype(np.float32),
        "w2": (n((K, N)) / np.sqrt(K) / s).astype(np.float32),
        "w3": (n((K, N)) / np.sqrt(K) / s).astype(np.float32),
        "hw": n((N, S)).astype(np.float32),
        "offs": striped(np.random.permutation(T)[:S]),
        "par": striped8(np.random.randint(0, S, (8, S))),
    }


def reference(x_words, x_scales, cell, w1, w2, w3, hw, offs, par):
    xq = unpack_weight(x_words, x_scales)[:, unstriped(offs)]
    rg = sigmoid(mxq(f64(w3), 0, "e4m3").T @ xq)
    y = mxq(f64(w1), 0, "e4m3").T @ xq
    fg = sigmoid(mxq(f64(w2), 0, "e4m3").T @ xq)
    c0 = f64(cell)[np.arange(N)[:, None], runs(par, N)]
    cn = y + fg * (c0 - y)
    out_0 = f64(hw) + rg * (np.tanh(cn) - f64(hw))
    return (out_0,) + planes(out_0)

@@ -1,0 +1,286 @@
+from contextlib import ExitStack
+
+import concourse.mybir as mybir
+
+K, T, S, N = 1024, 2048, 512, 512
+FLOPS = 3 * 2 * K * N * S
+
+F32 = mybir.dt.float32
+BF16 = mybir.dt.bfloat16
+I32 = mybir.dt.int32
+U32 = mybir.dt.uint32
+U16 = mybir.dt.uint16
+U8 = mybir.dt.uint8
+FP8X4 = mybir.dt.float8_e4m3fn_x4
+ALU = mybir.AluOpType
+SIGMOID = mybir.ActivationFunctionType.Sigmoid
+
+P = 128
+PACK = 4
+PASSES = K // (P * PACK)
+HALF = S // 2
+
+
+def tile_picked_sru8_none_po_kernel(
+    tc, x_words, x_scales, cell, w1, w2, w3, hw, offs, par, out_0, out_1, out_2
+):
+    nc = tc.nc
+    with ExitStack() as ctx:
+        lists = ctx.enter_context(tc.tile_pool(name="lists", bufs=1))
+        keep = ctx.enter_context(tc.tile_pool(name="keep", bufs=1))
+        psum = ctx.enter_context(tc.psum_pool(name="psum", bufs=1))
+
+        offs_sb = lists.tile([P, S // 16], U16, name="offs_sb")
+        par_sb = lists.tile([P, S // 16], U16, name="par_sb")
+
+        x_table = [keep.tile([P, T], U32, name=f"x_table{g}", align_bytes=64) for g in range(PASSES)]
+        x_codes = [keep.tile([P, S], U32, name=f"x_codes{g}", align_bytes=64) for g in range(PASSES)]
+        scale_table = keep.tile([P, T], U8, name="scale_table", align_bytes=64)
+        x_planes = keep.tile([P, S], U8, name="x_planes", align_bytes=64)
+        cell_sb = [keep.tile([P, S], F32, name=f"cell{t}", align_bytes=64) for t in range(PACK)]
+        hw_sb = keep.tile([P, PACK, S], F32, name="hw_sb")
+        raw = {}
+        rounded = {}
+        codes = {}
+        planes = {}
+        for name in ("w1", "w2", "w3"):
+            for g in range(PASSES):
+                raw[name, g] = keep.tile([P, PACK, N], F32, name=f"raw_{name}_{g}", align_bytes=64)
+                for h in range(2):
+                    rounded[name, g, h] = keep.tile([P, 2, P, PACK], BF16, name=f"rounded_{name}_{g}_{h}", align_bytes=64)
+                    codes[name, g, h] = keep.tile([P, 2 * P], U32, name=f"codes_{name}_{g}_{h}", align_bytes=64)
+                    planes[name, g, h] = keep.tile([P, 2 * P], U8, name=f"planes_{name}_{g}_{h}", align_bytes=64)
+        weights = {"w1": w1, "w2": w2, "w3": w3}
+
+        def load_w(name, g):
+            rows = weights[name][g * P * PACK : (g + 1) * P * PACK, :]
+            nc.sync.dma_start(out=raw[name, g][:], in_=rows.rearrange("(p j) c -> p j c", j=PACK))
+
+        def load_x(g):
+            nc.sync.dma_start(
+                out=x_table[g][:].bitcast(I32), in_=x_words[g].rearrange("p n t -> p (n t)").bitcast(I32)
+            )
+
+        nc.vector.memset(scale_table[:].bitcast(I32), 0)
+
+        load_w("w2", 0)
+        nc.sync.dma_start(offs_sb[:], offs)
+        load_x(0)
+        for q in range(4):
+            nc.sync.dma_start(
+                out=scale_table[32 * q : 32 * q + 4 * PASSES, :].bitcast(I32),
+                in_=x_scales[:, 4 * q : 4 * q + 4, :].bitcast(I32),
+            )
+        load_w("w2", 1)
+        nc.sync.dma_start(par_sb[:], par)
+        cell_rows = cell.rearrange("(p t) j -> p t j", t=PACK)
+        for t in range(PACK):
+            if t == 2:
+                load_x(1)
+            nc.sync.dma_start(out=cell_sb[t][:], in_=cell_rows[:, t, :])
+        load_w("w1", 0)
+        load_w("w1", 1)
+        load_w("w3", 0)
+        load_w("w3", 1)
+        nc.sync.dma_start(out=hw_sb[:], in_=hw.rearrange("(p t) j -> p t j", t=PACK))
+
+        def round_w(name, g, h, on_vector):
+            src = raw[name, g][:].rearrange("p j (m t) -> p m j t", t=PACK)[:, :, :, 2 * h : 2 * h + 2]
+            dst = rounded[name, g, h][:].rearrange("p t m j -> p m j t")
+            if on_vector:
+                nc.vector.tensor_copy(out=dst, in_=src)
+            else:
+                nc.scalar.copy(out=dst, in_=src)
+
+        def quantize_w(name, g, h):
+            nc.vector.quantize_mx(
+                out=codes[name, g, h][:].bitcast(FP8X4),
+                scales=planes[name, g, h][:],
+                in_=rounded[name, g, h][:].rearrange("p t m j -> p (t m j)"),
+            )
+
+        def multiply(name, g, t, bank):
+            cols = slice((t % 2) * P, (t % 2 + 1) * P)
+            nc.tensor.matmul_mx(
+                out=bank[:],
+                lhsT=codes[name, g, t // 2][:, cols].bitcast(FP8X4),
+                lhsT_scale=planes[name, g, t // 2][:, cols],
+                rhs=x_codes[g][:].bitcast(FP8X4),
+                rhs_scale=x_planes[4 * g : P, :],
+                start=(g == 0),
+                stop=(g == PASSES - 1),
+            )
+
+        def gather_x(g):
+            nc.vector.tensor_copy(out=x_codes[g][:], in_=x_table[g][:].indirect(offs_sb[:]))
+
+        def wide(name):
+            return keep.tile([P, PACK, S], F32, name=name, align_bytes=64)
+
+        fg = wide("fg")
+        kept = wide("kept")
+        fresh = wide("fresh")
+        cn = wide("cn")
+        sg = wide("sg")
+        lift = wide("lift")
+        rg = wide("rg")
+        mixed = wide("mixed")
+        result = wide("result")
+
+        c0 = wide("c0")
+
+        def gather_cell(t):
+            for h in range(2):
+                nc.vector.tensor_copy(
+                    out=c0[:, t, h * HALF : (h + 1) * HALF],
+                    in_=cell_sb[t][:].indirect(par_sb[:, h * HALF // 16 : (h + 1) * HALF // 16]),
+                )
+
+        def make_kept(t):
+            nc.vector.tensor_tensor(out=kept[:, t, :], in0=c0[:, t, :], in1=fg[:, t, :], op=ALU.mult)
+
+        def make_fresh(t):
+            nc.vector.scalar_tensor_tensor(
+                out=fresh[:, t, :], in0=fg[:, t, :], scalar=1.0, in1=y[t][:], op0=ALU.subtract, op1=ALU.mult
+            )
+
+        def make_cn(t):
+            nc.vector.tensor_tensor(out=cn[:, t, :], in0=kept[:, t, :], in1=fresh[:, t, :], op=ALU.subtract)
+
+        def make_sg(t):
+            nc.scalar.activation(out=sg[:, t, :], in_=cn[:, t, :], func=SIGMOID, scale=2.0)
+
+        def make_lift(t):
+            nc.vector.scalar_tensor_tensor(
+                out=lift[:, t, :], in0=sg[:, t, :], scalar=2.0, in1=hw_sb[:, t, :], op0=ALU.mult, op1=ALU.subtract
+            )
+
+        z2 = [psum.tile([P, S], F32, name=f"z2_{t}", tag=f"gate{t}") for t in range(PACK)]
+        for h in range(2):
+            round_w("w2", 0, h, False)
+        for h in range(2):
+            quantize_w("w2", 0, h)
+        gather_x(0)
+        nc.vector.tensor_copy(out=x_planes[:], in_=scale_table[:].indirect(offs_sb[:]))
+        for t in range(PACK):
+            multiply("w2", 0, t, z2[t])
+        for h in range(2):
+            round_w("w2", 1, h, False)
+        gather_cell(0)
+        quantize_w("w2", 1, 0)
+        gather_cell(1)
+        quantize_w("w2", 1, 1)
+        gather_x(1)
+        for t in range(PACK):
+            multiply("w2", 1, t, z2[t])
+            nc.scalar.activation(out=fg[:, t, :], in_=z2[t][:], func=SIGMOID)
+        gather_cell(2)
+        gather_cell(3)
+        for t in range(PACK):
+            make_kept(t)
+
+        y = [psum.tile([P, S], F32, name=f"y_{t}", tag=f"cand{t}") for t in range(PACK)]
+        z3 = [psum.tile([P, S], F32, name=f"z3_{t}", tag=f"gate{t}") for t in range(PACK)]
+        round_w("w1", 0, 0, False)
+        round_w("w1", 0, 1, False)
+        round_w("w1", 1, 0, True)
+        round_w("w1", 1, 1, False)
+        for h in range(2):
+            for g in range(PASSES):
+                quantize_w("w1", g, h)
+            for t in (2 * h, 2 * h + 1):
+                for g in range(PASSES):
+                    multiply("w1", g, t, y[t])
+        for g in range(PASSES):
+            for h in range(2):
+                round_w("w3", g, h, False)
+        make_fresh(0)
+        make_fresh(1)
+        make_cn(0)
+        make_fresh(2)
+        make_cn(1)
+        make_fresh(3)
+        make_cn(2)
+        quantize_w("w3", 0, 0)
+        make_cn(3)
+        quantize_w("w3", 0, 1)
+        for t in range(PACK):
+            multiply("w3", 0, t, z3[t])
+        for h in range(2):
+            quantize_w("w3", 1, h)
+        for t in range(PACK):
+            multiply("w3", 1, t, z3[t])
+        for t in range(PACK):
+            make_sg(t)
+            make_lift(t)
+
+        out_bf = keep.tile([P, S, PACK], BF16, name="out_bf", align_bytes=64)
+        out_codes = keep.tile([P, S], U32, name="out_codes", align_bytes=64)
+        out_plane = keep.tile([P, S], U8, name="out_plane", align_bytes=64)
+        out_rows = out_0.rearrange("(p t) j -> p t j", t=PACK)
+        word_rows = out_1[0].rearrange("p n t -> p (n t)").bitcast(I32)
+
+        for h in range(2):
+            cols = slice(h * HALF, (h + 1) * HALF)
+            for t in range(PACK):
+                nc.scalar.activation(out=rg[:, t, cols], in_=z3[t][:, cols], func=SIGMOID)
+
+        def make_mixed(ts, cols):
+            nc.vector.scalar_tensor_tensor(
+                out=mixed[:, ts, cols], in0=lift[:, ts, cols], scalar=1.0, in1=rg[:, ts, cols],
+                op0=ALU.subtract, op1=ALU.mult,
+            )
+
+        def make_result(ts, cols):
+            nc.vector.tensor_tensor(
+                out=result[:, ts, cols], in0=mixed[:, ts, cols], in1=hw_sb[:, ts, cols], op=ALU.add
+            )
+
+        def store_result(cols):
+            nc.sync.dma_start(out=out_rows[:, :, cols], in_=result[:, :, cols])
+
+        def round_result(cols, on_vector):
+            dst = out_bf[:, cols, :].rearrange("p (c i) t -> p c t i", i=4)
+            src = result[:, :, cols].rearrange("p t (c i) -> p c t i", i=4)
+            if on_vector:
+                nc.vector.tensor_copy(out=dst, in_=src)
+            else:
+                nc.scalar.copy(out=dst, in_=src)
+
+        def quantize_result(cols):
+            nc.vector.quantize_mx(
+                out=out_codes[:, cols].bitcast(FP8X4),
+                scales=out_plane[:, cols],
+                in_=out_bf[:, cols, :].rearrange("p c t -> p (c t)"),
+            )
+
+        def store_words(cols):
+            nc.sync.dma_start(out=word_rows[:, cols], in_=out_codes[:, cols].bitcast(I32))
+
+        first, second, third = slice(0, 256), slice(256, 384), slice(384, 512)
+        low, high, every = slice(0, 2), slice(2, 4), slice(0, 4)
+        make_mixed(low, first)
+        make_mixed(high, first)
+        make_result(low, first)
+        make_result(high, first)
+        store_result(first)
+        round_result(first, False)
+        make_mixed(every, second)
+        make_mixed(every, third)
+        make_result(every, second)
+        store_result(second)
+        round_result(second, False)
+        quantize_result(first)
+        store_words(first)
+        make_result(every, third)
+        store_result(third)
+        quantize_result(second)
+        round_result(third, True)
+        quantize_result(third)
+        store_words(slice(256, 512))
+        for q in range(4):
+            queue = nc.sync if q % 2 == 0 else nc.scalar
+            queue.dma_start(
+                out=out_2[0, 4 * q : 4 * q + 4, :].bitcast(I32),
+                in_=out_plane[32 * q : 32 * q + 4, :].bitcast(I32),
+            )

@@ -1,6 +1,7 @@
 from contextlib import ExitStack
 
 import concourse.mybir as mybir
+from concourse.masks import make_identity
 
 K, T, S, N = 1024, 2048, 512, 512
 FLOPS = 3 * 2 * K * N * S
@@ -14,6 +15,8 @@ U8 = mybir.dt.uint8
 FP8X4 = mybir.dt.float8_e4m3fn_x4
 ALU = mybir.AluOpType
 SIGMOID = mybir.ActivationFunctionType.Sigmoid
+TANH = mybir.ActivationFunctionType.Tanh
+COPY = mybir.ActivationFunctionType.Copy
 
 P = 128
 PACK = 4
@@ -63,31 +66,41 @@ def tile_picked_sru8_none_po_kernel(
 
         nc.vector.memset(scale_table[:].bitcast(I32), 0)
 
+        identity = keep.tile([P, P], F32, name="identity")
+        make_identity(nc, identity[:])
+
+        cell_rows = cell.rearrange("(p t) j -> p t j", t=PACK)
+        hw_rows = hw.rearrange("(p t) j -> p t j", t=PACK)
+        nc.sync.dma_start(par_sb[:], par)
+        for t in (0, 1):
+            nc.sync.dma_start(out=cell_sb[t][:], in_=cell_rows[:, t, :])
         load_w("w2", 0)
-        nc.sync.dma_start(offs_sb[:], offs)
-        load_x(0)
         for q in range(4):
             nc.sync.dma_start(
                 out=scale_table[32 * q : 32 * q + 4 * PASSES, :].bitcast(I32),
                 in_=x_scales[:, 4 * q : 4 * q + 4, :].bitcast(I32),
             )
+        nc.sync.dma_start(offs_sb[:], offs)
+        load_x(0)
         load_w("w2", 1)
-        nc.sync.dma_start(par_sb[:], par)
-        cell_rows = cell.rearrange("(p t) j -> p t j", t=PACK)
-        for t in range(PACK):
-            if t == 2:
-                load_x(1)
+        load_x(1)
+        for t in (2, 3):
             nc.sync.dma_start(out=cell_sb[t][:], in_=cell_rows[:, t, :])
         load_w("w1", 0)
         load_w("w1", 1)
         load_w("w3", 0)
         load_w("w3", 1)
-        nc.sync.dma_start(out=hw_sb[:], in_=hw.rearrange("(p t) j -> p t j", t=PACK))
+        for h in range(2):
+            nc.sync.dma_start(out=hw_sb[:, 2 * h : 2 * h + 2, :], in_=hw_rows[:, 2 * h : 2 * h + 2, :])
 
         def round_w(name, g, h, on_vector):
             src = raw[name, g][:].rearrange("p j (m t) -> p m j t", t=PACK)[:, :, :, 2 * h : 2 * h + 2]
             dst = rounded[name, g, h][:].rearrange("p t m j -> p m j t")
-            if on_vector:
+            if name == "w1" and on_vector:
+                nc.vector.tensor_scalar(out=dst, in0=src, scalar1=-1.0, scalar2=None, op0=ALU.mult)
+            elif name == "w1":
+                nc.scalar.activation(out=dst, in_=src, func=COPY, scale=-1.0)
+            elif on_vector:
                 nc.vector.tensor_copy(out=dst, in_=src)
             else:
                 nc.scalar.copy(out=dst, in_=src)
@@ -120,7 +133,6 @@ def tile_picked_sru8_none_po_kernel(
         fg = wide("fg")
         kept = wide("kept")
         fresh = wide("fresh")
-        cn = wide("cn")
         sg = wide("sg")
         lift = wide("lift")
         rg = wide("rg")
@@ -144,43 +156,45 @@ def tile_picked_sru8_none_po_kernel(
                 out=fresh[:, t, :], in0=fg[:, t, :], scalar=1.0, in1=y[t][:], op0=ALU.subtract, op1=ALU.mult
             )
 
-        def make_cn(t):
-            nc.vector.tensor_tensor(out=cn[:, t, :], in0=kept[:, t, :], in1=fresh[:, t, :], op=ALU.subtract)
+        def turn(bank, src, t, first, last):
+            for b in range(PACK):
+                cols = slice(b * P, (b + 1) * P)
+                nc.tensor.matmul(
+                    out=bank[:, cols], lhsT=src[:, t, cols], rhs=identity[:], is_transpose=True,
+                    start=(first and b == 0), stop=(last and b == PACK - 1),
+                )
 
         def make_sg(t):
-            nc.scalar.activation(out=sg[:, t, :], in_=cn[:, t, :], func=SIGMOID, scale=2.0)
+            nc.scalar.activation(out=sg[:, t, :], in_=cn_turned[t][:], func=TANH)
+            turn(th[t], sg, t, True, True)
 
         def make_lift(t):
-            nc.vector.scalar_tensor_tensor(
-                out=lift[:, t, :], in0=sg[:, t, :], scalar=2.0, in1=hw_sb[:, t, :], op0=ALU.mult, op1=ALU.subtract
-            )
+            nc.vector.tensor_tensor(out=lift[:, t, :], in0=th[t][:], in1=hw_sb[:, t, :], op=ALU.subtract)
 
         z2 = [psum.tile([P, S], F32, name=f"z2_{t}", tag=f"gate{t}") for t in range(PACK)]
+        gather_cell(0)
+        gather_cell(1)
+        nc.vector.tensor_copy(out=x_planes[:], in_=scale_table[:].indirect(offs_sb[:]))
         for h in range(2):
             round_w("w2", 0, h, False)
+        gather_x(0)
         for h in range(2):
             quantize_w("w2", 0, h)
-        gather_x(0)
-        nc.vector.tensor_copy(out=x_planes[:], in_=scale_table[:].indirect(offs_sb[:]))
         for t in range(PACK):
             multiply("w2", 0, t, z2[t])
         for h in range(2):
-            round_w("w2", 1, h, False)
-        gather_cell(0)
-        quantize_w("w2", 1, 0)
-        gather_cell(1)
-        quantize_w("w2", 1, 1)
+            round_w("w2", 1, h, h == 0)
+        for h in range(2):
+            quantize_w("w2", 1, h)
         gather_x(1)
         for t in range(PACK):
             multiply("w2", 1, t, z2[t])
             nc.scalar.activation(out=fg[:, t, :], in_=z2[t][:], func=SIGMOID)
         gather_cell(2)
         gather_cell(3)
-        for t in range(PACK):
-            make_kept(t)
 
         y = [psum.tile([P, S], F32, name=f"y_{t}", tag=f"cand{t}") for t in range(PACK)]
-        z3 = [psum.tile([P, S], F32, name=f"z3_{t}", tag=f"gate{t}") for t in range(PACK)]
+        cn_turned = [psum.tile([P, S], F32, name=f"cn_{t}", tag=f"gate{t}") for t in range(PACK)]
         round_w("w1", 0, 0, False)
         round_w("w1", 0, 1, False)
         round_w("w1", 1, 0, True)
@@ -191,28 +205,35 @@ def tile_picked_sru8_none_po_kernel(
             for t in (2 * h, 2 * h + 1):
                 for g in range(PASSES):
                     multiply("w1", g, t, y[t])
-        for g in range(PASSES):
-            for h in range(2):
-                round_w("w3", g, h, False)
-        make_fresh(0)
-        make_fresh(1)
-        make_cn(0)
-        make_fresh(2)
-        make_cn(1)
-        make_fresh(3)
-        make_cn(2)
-        quantize_w("w3", 0, 0)
-        make_cn(3)
-        quantize_w("w3", 0, 1)
+        for t in range(PACK):
+            make_kept(t)
+            turn(cn_turned[t], kept, t, True, False)
+        for t in range(PACK):
+            make_fresh(t)
+            turn(cn_turned[t], fresh, t, False, True)
+
+        z3 = [psum.tile([P, S], F32, name=f"z3_{t}", tag=f"cand{t}") for t in range(PACK)]
+        th = [psum.tile([P, S], F32, name=f"th_{t}", tag=f"gate{t}") for t in range(PACK)]
+        for h in range(2):
+            round_w("w3", 0, h, False)
+        make_sg(0)
+        make_sg(1)
+        round_w("w3", 1, 0, True)
+        round_w("w3", 1, 1, False)
+        for h in range(2):
+            quantize_w("w3", 0, h)
         for t in range(PACK):
             multiply("w3", 0, t, z3[t])
-        for h in range(2):
-            quantize_w("w3", 1, h)
+        make_sg(2)
+        make_sg(3)
+        quantize_w("w3", 1, 0)
+        make_lift(0)
+        make_lift(1)
+        quantize_w("w3", 1, 1)
         for t in range(PACK):
             multiply("w3", 1, t, z3[t])
-        for t in range(PACK):
-            make_sg(t)
-            make_lift(t)
+        make_lift(2)
+        make_lift(3)
 
         out_bf = keep.tile([P, S, PACK], BF16, name="out_bf", align_bytes=64)
         out_codes = keep.tile([P, S], U32, name="out_codes", align_bytes=64)
@@ -226,9 +247,8 @@ def tile_picked_sru8_none_po_kernel(
                 nc.scalar.activation(out=rg[:, t, cols], in_=z3[t][:, cols], func=SIGMOID)
 
         def make_mixed(ts, cols):
-            nc.vector.scalar_tensor_tensor(
-                out=mixed[:, ts, cols], in0=lift[:, ts, cols], scalar=1.0, in1=rg[:, ts, cols],
-                op0=ALU.subtract, op1=ALU.mult,
+            nc.vector.tensor_tensor(
+                out=mixed[:, ts, cols], in0=lift[:, ts, cols], in1=rg[:, ts, cols], op=ALU.mult
             )
 
         def make_result(ts, cols):

@@ -64,6 +64,13 @@ def tile_picked_sru8_none_po_kernel(
                 out=x_table[g][:].bitcast(I32), in_=x_words[g].rearrange("p n t -> p (n t)").bitcast(I32)
             )
 
+        def load_scales(g):
+            for q in range(4):
+                nc.sync.dma_start(
+                    out=scale_table[32 * q + 4 * g : 32 * q + 4 * g + 4, :].bitcast(I32),
+                    in_=x_scales[g, 4 * q : 4 * q + 4, :].bitcast(I32),
+                )
+
         nc.vector.memset(scale_table[:].bitcast(I32), 0)
 
         identity = keep.tile([P, P], F32, name="identity")
@@ -72,19 +79,16 @@ def tile_picked_sru8_none_po_kernel(
         cell_rows = cell.rearrange("(p t) j -> p t j", t=PACK)
         hw_rows = hw.rearrange("(p t) j -> p t j", t=PACK)
         nc.sync.dma_start(par_sb[:], par)
-        for t in (0, 1):
+        for t in range(2):
             nc.sync.dma_start(out=cell_sb[t][:], in_=cell_rows[:, t, :])
         load_w("w2", 0)
-        for q in range(4):
-            nc.sync.dma_start(
-                out=scale_table[32 * q : 32 * q + 4 * PASSES, :].bitcast(I32),
-                in_=x_scales[:, 4 * q : 4 * q + 4, :].bitcast(I32),
-            )
+        load_scales(0)
         nc.sync.dma_start(offs_sb[:], offs)
         load_x(0)
+        load_scales(1)
         load_w("w2", 1)
         load_x(1)
-        for t in (2, 3):
+        for t in range(2, PACK):
             nc.sync.dma_start(out=cell_sb[t][:], in_=cell_rows[:, t, :])
         load_w("w1", 0)
         load_w("w1", 1)
@@ -172,8 +176,8 @@ def tile_picked_sru8_none_po_kernel(
             nc.vector.tensor_tensor(out=lift[:, t, :], in0=th[t][:], in1=hw_sb[:, t, :], op=ALU.subtract)
 
         z2 = [psum.tile([P, S], F32, name=f"z2_{t}", tag=f"gate{t}") for t in range(PACK)]
-        gather_cell(0)
-        gather_cell(1)
+        for t in range(2):
+            gather_cell(t)
         nc.vector.tensor_copy(out=x_planes[:], in_=scale_table[:].indirect(offs_sb[:]))
         for h in range(2):
             round_w("w2", 0, h, False)
@@ -190,8 +194,8 @@ def tile_picked_sru8_none_po_kernel(
         for t in range(PACK):
             multiply("w2", 1, t, z2[t])
             nc.scalar.activation(out=fg[:, t, :], in_=z2[t][:], func=SIGMOID)
-        gather_cell(2)
-        gather_cell(3)
+        for t in range(2, PACK):
+            gather_cell(t)
 
         y = [psum.tile([P, S], F32, name=f"y_{t}", tag=f"cand{t}") for t in range(PACK)]
         cn_turned = [psum.tile([P, S], F32, name=f"cn_{t}", tag=f"gate{t}") for t in range(PACK)]

@@ -21,7 +21,10 @@ COPY = mybir.ActivationFunctionType.Copy
 P = 128
 PACK = 4
 PASSES = K // (P * PACK)
+QUADRANTS = P // 32
+PAIRS = PACK // 2
 HALF = S // 2
+EARLY_SLOTS = 2
 
 
 def tile_picked_sru8_none_po_kernel(
@@ -33,73 +36,73 @@ def tile_picked_sru8_none_po_kernel(
         keep = ctx.enter_context(tc.tile_pool(name="keep", bufs=1))
         psum = ctx.enter_context(tc.psum_pool(name="psum", bufs=1))
 
+        def slotted(name):
+            return keep.tile([P, PACK, S], F32, name=name, align_bytes=64)
+
+        def banks(name, tag):
+            return [psum.tile([P, S], F32, name=f"{name}{t}", tag=f"{tag}{t}") for t in range(PACK)]
+
         offs_sb = lists.tile([P, S // 16], U16, name="offs_sb")
         par_sb = lists.tile([P, S // 16], U16, name="par_sb")
-
-        x_table = [keep.tile([P, T], U32, name=f"x_table{g}", align_bytes=64) for g in range(PASSES)]
-        x_codes = [keep.tile([P, S], U32, name=f"x_codes{g}", align_bytes=64) for g in range(PASSES)]
+        word_table = [keep.tile([P, T], U32, name=f"word_table{g}", align_bytes=64) for g in range(PASSES)]
         scale_table = keep.tile([P, T], U8, name="scale_table", align_bytes=64)
+        x_codes = [keep.tile([P, S], U32, name=f"x_codes{g}", align_bytes=64) for g in range(PASSES)]
         x_planes = keep.tile([P, S], U8, name="x_planes", align_bytes=64)
-        cell_sb = [keep.tile([P, S], F32, name=f"cell{t}", align_bytes=64) for t in range(PACK)]
-        hw_sb = keep.tile([P, PACK, S], F32, name="hw_sb")
-        raw = {}
-        rounded = {}
-        codes = {}
-        planes = {}
-        for name in ("w1", "w2", "w3"):
+        cell_table = [keep.tile([P, S], F32, name=f"cell_table{t}", align_bytes=64) for t in range(PACK)]
+        hw_sb = slotted("hw_sb")
+        identity = keep.tile([P, P], F32, name="identity")
+
+        weights = {"w1": w1, "w2": w2, "w3": w3}
+        raw, rounded, codes, planes = {}, {}, {}, {}
+        for name in weights:
             for g in range(PASSES):
                 raw[name, g] = keep.tile([P, PACK, N], F32, name=f"raw_{name}_{g}", align_bytes=64)
-                for h in range(2):
-                    rounded[name, g, h] = keep.tile([P, 2, P, PACK], BF16, name=f"rounded_{name}_{g}_{h}", align_bytes=64)
-                    codes[name, g, h] = keep.tile([P, 2 * P], U32, name=f"codes_{name}_{g}_{h}", align_bytes=64)
-                    planes[name, g, h] = keep.tile([P, 2 * P], U8, name=f"planes_{name}_{g}_{h}", align_bytes=64)
-        weights = {"w1": w1, "w2": w2, "w3": w3}
 
-        def load_w(name, g):
+        cell_rows = cell.rearrange("(p t) j -> p t j", t=PACK)
+        hw_rows = hw.rearrange("(p t) j -> p t j", t=PACK)
+
+        def load_weight(name, g):
             rows = weights[name][g * P * PACK : (g + 1) * P * PACK, :]
-            nc.sync.dma_start(out=raw[name, g][:], in_=rows.rearrange("(p j) c -> p j c", j=PACK))
+            nc.sync.dma_start(out=raw[name, g][:], in_=rows.rearrange("(p i) c -> p i c", i=PACK))
 
-        def load_x(g):
+        def load_words(g):
             nc.sync.dma_start(
-                out=x_table[g][:].bitcast(I32), in_=x_words[g].rearrange("p n t -> p (n t)").bitcast(I32)
+                out=word_table[g][:].bitcast(I32), in_=x_words[g].rearrange("p n i -> p (n i)").bitcast(I32)
             )
 
         def load_scales(g):
-            for q in range(4):
+            for q in range(QUADRANTS):
                 nc.sync.dma_start(
                     out=scale_table[32 * q + 4 * g : 32 * q + 4 * g + 4, :].bitcast(I32),
                     in_=x_scales[g, 4 * q : 4 * q + 4, :].bitcast(I32),
                 )
 
         nc.vector.memset(scale_table[:].bitcast(I32), 0)
-
-        identity = keep.tile([P, P], F32, name="identity")
         make_identity(nc, identity[:])
 
-        cell_rows = cell.rearrange("(p t) j -> p t j", t=PACK)
-        hw_rows = hw.rearrange("(p t) j -> p t j", t=PACK)
         nc.sync.dma_start(par_sb[:], par)
-        for t in range(2):
-            nc.sync.dma_start(out=cell_sb[t][:], in_=cell_rows[:, t, :])
-        load_w("w2", 0)
+        for t in range(EARLY_SLOTS):
+            nc.sync.dma_start(out=cell_table[t][:], in_=cell_rows[:, t, :])
+        load_weight("w2", 0)
         load_scales(0)
         nc.sync.dma_start(offs_sb[:], offs)
-        load_x(0)
+        load_words(0)
         load_scales(1)
-        load_w("w2", 1)
-        load_x(1)
-        for t in range(2, PACK):
-            nc.sync.dma_start(out=cell_sb[t][:], in_=cell_rows[:, t, :])
-        load_w("w1", 0)
-        load_w("w1", 1)
-        load_w("w3", 0)
-        load_w("w3", 1)
-        for h in range(2):
+        load_weight("w2", 1)
+        load_words(1)
+        for t in range(EARLY_SLOTS, PACK):
+            nc.sync.dma_start(out=cell_table[t][:], in_=cell_rows[:, t, :])
+        for name in ("w1", "w3"):
+            for g in range(PASSES):
+                load_weight(name, g)
+        for h in range(PAIRS):
             nc.sync.dma_start(out=hw_sb[:, 2 * h : 2 * h + 2, :], in_=hw_rows[:, 2 * h : 2 * h + 2, :])
 
-        def round_w(name, g, h, on_vector):
-            src = raw[name, g][:].rearrange("p j (m t) -> p m j t", t=PACK)[:, :, :, 2 * h : 2 * h + 2]
-            dst = rounded[name, g, h][:].rearrange("p t m j -> p m j t")
+        def round_weight(name, g, h, on_vector):
+            tag = f"rounded_{name}_{g}_{h}"
+            rounded[name, g, h] = keep.tile([P, 2, P, PACK], BF16, name=tag, tag=tag, align_bytes=64)
+            src = raw[name, g][:].rearrange("p i (m t) -> p m i t", t=PACK)[:, :, :, 2 * h : 2 * h + 2]
+            dst = rounded[name, g, h][:].rearrange("p s m i -> p m i s")
             if name == "w1" and on_vector:
                 nc.vector.tensor_scalar(out=dst, in0=src, scalar1=-1.0, scalar2=None, op0=ALU.mult)
             elif name == "w1":
@@ -109,12 +112,17 @@ def tile_picked_sru8_none_po_kernel(
             else:
                 nc.scalar.copy(out=dst, in_=src)
 
-        def quantize_w(name, g, h):
+        def quantize_weight(name, g, h, codes_tag):
+            codes[name, g, h] = keep.tile([P, 2 * P], U32, name=f"codes_{name}_{g}_{h}", tag=codes_tag, align_bytes=64)
+            planes[name, g, h] = keep.tile([P, 2 * P], U8, name=f"planes_{name}_{g}_{h}", align_bytes=64)
             nc.vector.quantize_mx(
                 out=codes[name, g, h][:].bitcast(FP8X4),
                 scales=planes[name, g, h][:],
-                in_=rounded[name, g, h][:].rearrange("p t m j -> p (t m j)"),
+                in_=rounded[name, g, h][:].rearrange("p s m i -> p (s m i)"),
             )
+
+        def quantize(name, g, h):
+            quantize_weight(name, g, h, f"codes_{name}_{g}_{h}")
 
         def multiply(name, g, t, bank):
             cols = slice((t % 2) * P, (t % 2 + 1) * P)
@@ -128,143 +136,141 @@ def tile_picked_sru8_none_po_kernel(
                 stop=(g == PASSES - 1),
             )
 
-        def gather_x(g):
-            nc.vector.tensor_copy(out=x_codes[g][:], in_=x_table[g][:].indirect(offs_sb[:]))
-
-        def wide(name):
-            return keep.tile([P, PACK, S], F32, name=name, align_bytes=64)
-
-        fg = wide("fg")
-        kept = wide("kept")
-        fresh = wide("fresh")
-        sg = wide("sg")
-        lift = wide("lift")
-        rg = wide("rg")
-        mixed = wide("mixed")
-        result = wide("result")
-
-        c0 = wide("c0")
-
-        def gather_cell(t):
-            for h in range(2):
-                nc.vector.tensor_copy(
-                    out=c0[:, t, h * HALF : (h + 1) * HALF],
-                    in_=cell_sb[t][:].indirect(par_sb[:, h * HALF // 16 : (h + 1) * HALF // 16]),
-                )
-
-        def make_kept(t):
-            nc.vector.tensor_tensor(out=kept[:, t, :], in0=c0[:, t, :], in1=fg[:, t, :], op=ALU.mult)
-
-        def make_fresh(t):
-            nc.vector.scalar_tensor_tensor(
-                out=fresh[:, t, :], in0=fg[:, t, :], scalar=1.0, in1=y[t][:], op0=ALU.subtract, op1=ALU.mult
-            )
-
-        def turn(bank, src, t, first, last):
-            for b in range(PACK):
+        def turn(bank, row, first, last):
+            for b in range(S // P):
                 cols = slice(b * P, (b + 1) * P)
                 nc.tensor.matmul(
-                    out=bank[:, cols], lhsT=src[:, t, cols], rhs=identity[:], is_transpose=True,
-                    start=(first and b == 0), stop=(last and b == PACK - 1),
+                    out=bank[:, cols],
+                    lhsT=row[:, cols],
+                    rhs=identity[:],
+                    is_transpose=True,
+                    start=(first and b == 0),
+                    stop=(last and b == S // P - 1),
                 )
 
-        def make_sg(t):
-            nc.scalar.activation(out=sg[:, t, :], in_=cn_turned[t][:], func=TANH)
-            turn(th[t], sg, t, True, True)
+        c0 = slotted("c0")
 
-        def make_lift(t):
-            nc.vector.tensor_tensor(out=lift[:, t, :], in0=th[t][:], in1=hw_sb[:, t, :], op=ALU.subtract)
+        def gather_words(g):
+            nc.vector.tensor_copy(out=x_codes[g][:], in_=word_table[g][:].indirect(offs_sb[:]))
 
-        z2 = [psum.tile([P, S], F32, name=f"z2_{t}", tag=f"gate{t}") for t in range(PACK)]
-        for t in range(2):
+        def gather_cell(t):
+            for first in (0, HALF):
+                nc.vector.tensor_copy(
+                    out=c0[:, t, first : first + HALF],
+                    in_=cell_table[t][:].indirect(par_sb[:, first // 16 : (first + HALF) // 16]),
+                )
+
+        fg = slotted("fg")
+        z2 = banks("z2_", "gate")
+        for t in range(EARLY_SLOTS):
             gather_cell(t)
         nc.vector.tensor_copy(out=x_planes[:], in_=scale_table[:].indirect(offs_sb[:]))
-        for h in range(2):
-            round_w("w2", 0, h, False)
-        gather_x(0)
-        for h in range(2):
-            quantize_w("w2", 0, h)
+        for h in range(PAIRS):
+            round_weight("w2", 0, h, False)
+        gather_words(0)
+        for h in range(PAIRS):
+            quantize("w2", 0, h)
         for t in range(PACK):
             multiply("w2", 0, t, z2[t])
-        for h in range(2):
-            round_w("w2", 1, h, h == 0)
-        for h in range(2):
-            quantize_w("w2", 1, h)
-        gather_x(1)
+        for h in range(PAIRS):
+            round_weight("w2", 1, h, h == 0)
+        for h in range(PAIRS):
+            quantize("w2", 1, h)
+        gather_words(1)
         for t in range(PACK):
             multiply("w2", 1, t, z2[t])
             nc.scalar.activation(out=fg[:, t, :], in_=z2[t][:], func=SIGMOID)
-        for t in range(2, PACK):
+        for t in range(EARLY_SLOTS, PACK):
             gather_cell(t)
 
-        y = [psum.tile([P, S], F32, name=f"y_{t}", tag=f"cand{t}") for t in range(PACK)]
-        cn_turned = [psum.tile([P, S], F32, name=f"cn_{t}", tag=f"gate{t}") for t in range(PACK)]
-        round_w("w1", 0, 0, False)
-        round_w("w1", 0, 1, False)
-        round_w("w1", 1, 0, True)
-        round_w("w1", 1, 1, False)
-        for h in range(2):
+        kept = slotted("kept")
+        fresh = slotted("fresh")
+        neg_y = banks("neg_y", "candidate")
+        cn_turned = banks("cn_turned", "gate")
+        for h in range(PAIRS):
+            round_weight("w1", 0, h, False)
+        quantize("w1", 0, 0)
+        for t in (0, 1):
+            multiply("w1", 0, t, neg_y[t])
+        for h in range(PAIRS):
+            round_weight("w1", 1, h, h == 0)
+        quantize("w1", 1, 0)
+        for t in (0, 1):
+            multiply("w1", 1, t, neg_y[t])
+        quantize_weight("w1", 0, 1, "rounded_w1_1_0")
+        quantize("w1", 1, 1)
+        for t in (2, 3):
             for g in range(PASSES):
-                quantize_w("w1", g, h)
-            for t in (2 * h, 2 * h + 1):
-                for g in range(PASSES):
-                    multiply("w1", g, t, y[t])
+                multiply("w1", g, t, neg_y[t])
         for t in range(PACK):
-            make_kept(t)
-            turn(cn_turned[t], kept, t, True, False)
+            nc.vector.tensor_tensor(out=kept[:, t, :], in0=c0[:, t, :], in1=fg[:, t, :], op=ALU.mult)
+            turn(cn_turned[t], kept[:, t, :], True, False)
         for t in range(PACK):
-            make_fresh(t)
-            turn(cn_turned[t], fresh, t, False, True)
+            nc.vector.scalar_tensor_tensor(
+                out=fresh[:, t, :], in0=fg[:, t, :], scalar=1.0, in1=neg_y[t][:], op0=ALU.subtract, op1=ALU.mult
+            )
+            turn(cn_turned[t], fresh[:, t, :], False, True)
 
-        z3 = [psum.tile([P, S], F32, name=f"z3_{t}", tag=f"cand{t}") for t in range(PACK)]
-        th = [psum.tile([P, S], F32, name=f"th_{t}", tag=f"gate{t}") for t in range(PACK)]
-        for h in range(2):
-            round_w("w3", 0, h, False)
-        make_sg(0)
-        make_sg(1)
-        round_w("w3", 1, 0, True)
-        round_w("w3", 1, 1, False)
-        for h in range(2):
-            quantize_w("w3", 0, h)
+        tanh_turned = slotted("tanh_turned")
+        gap = slotted("gap")
+        z3 = banks("z3_", "candidate")
+        tanh_cn = banks("tanh_cn", "gate")
+
+        def make_tanh(t):
+            nc.scalar.activation(out=tanh_turned[:, t, :], in_=cn_turned[t][:], func=TANH)
+            turn(tanh_cn[t], tanh_turned[:, t, :], True, True)
+
+        def make_gap(t):
+            nc.vector.tensor_tensor(out=gap[:, t, :], in0=tanh_cn[t][:], in1=hw_sb[:, t, :], op=ALU.subtract)
+
+        for h in range(PAIRS):
+            round_weight("w3", 0, h, False)
+        for t in (0, 1):
+            make_tanh(t)
+        for h in range(PAIRS):
+            quantize("w3", 0, h)
         for t in range(PACK):
             multiply("w3", 0, t, z3[t])
-        make_sg(2)
-        make_sg(3)
-        quantize_w("w3", 1, 0)
-        make_lift(0)
-        make_lift(1)
-        quantize_w("w3", 1, 1)
-        for t in range(PACK):
-            multiply("w3", 1, t, z3[t])
-        make_lift(2)
-        make_lift(3)
+        for h in range(PAIRS):
+            round_weight("w3", 1, h, h == 0)
+        for t in (2, 3):
+            make_tanh(t)
+        for h in range(PAIRS):
+            quantize("w3", 1, h)
+            for t in (2 * h, 2 * h + 1):
+                multiply("w3", 1, t, z3[t])
+            for t in (2 * h, 2 * h + 1):
+                make_gap(t)
 
-        out_bf = keep.tile([P, S, PACK], BF16, name="out_bf", align_bytes=64)
-        out_codes = keep.tile([P, S], U32, name="out_codes", align_bytes=64)
-        out_plane = keep.tile([P, S], U8, name="out_plane", align_bytes=64)
+        rg = slotted("rg")
+        mixed = slotted("mixed")
+        result = slotted("result")
+        result_bf16 = keep.tile([P, S, PACK], BF16, name="result_bf16", align_bytes=64)
+        result_codes = keep.tile([P, S], U32, name="result_codes", align_bytes=64)
+        result_plane = keep.tile([P, S], U8, name="result_plane", align_bytes=64)
         out_rows = out_0.rearrange("(p t) j -> p t j", t=PACK)
-        word_rows = out_1[0].rearrange("p n t -> p (n t)").bitcast(I32)
+        word_rows = out_1[0].rearrange("p n i -> p (n i)").bitcast(I32)
 
-        for h in range(2):
-            cols = slice(h * HALF, (h + 1) * HALF)
+        for first in (0, HALF):
             for t in range(PACK):
+                cols = slice(first, first + HALF)
                 nc.scalar.activation(out=rg[:, t, cols], in_=z3[t][:, cols], func=SIGMOID)
 
-        def make_mixed(ts, cols):
+        def make_mixed(slots, cols):
             nc.vector.tensor_tensor(
-                out=mixed[:, ts, cols], in0=lift[:, ts, cols], in1=rg[:, ts, cols], op=ALU.mult
+                out=mixed[:, slots, cols], in0=gap[:, slots, cols], in1=rg[:, slots, cols], op=ALU.mult
             )
 
-        def make_result(ts, cols):
+        def make_result(slots, cols):
             nc.vector.tensor_tensor(
-                out=result[:, ts, cols], in0=mixed[:, ts, cols], in1=hw_sb[:, ts, cols], op=ALU.add
+                out=result[:, slots, cols], in0=mixed[:, slots, cols], in1=hw_sb[:, slots, cols], op=ALU.add
             )
 
         def store_result(cols):
             nc.sync.dma_start(out=out_rows[:, :, cols], in_=result[:, :, cols])
 
         def round_result(cols, on_vector):
-            dst = out_bf[:, cols, :].rearrange("p (c i) t -> p c t i", i=4)
+            dst = result_bf16[:, cols, :].rearrange("p (c i) t -> p c t i", i=4)
             src = result[:, :, cols].rearrange("p t (c i) -> p c t i", i=4)
             if on_vector:
                 nc.vector.tensor_copy(out=dst, in_=src)
@@ -273,38 +279,39 @@ def tile_picked_sru8_none_po_kernel(
 
         def quantize_result(cols):
             nc.vector.quantize_mx(
-                out=out_codes[:, cols].bitcast(FP8X4),
-                scales=out_plane[:, cols],
-                in_=out_bf[:, cols, :].rearrange("p c t -> p (c t)"),
+                out=result_codes[:, cols].bitcast(FP8X4),
+                scales=result_plane[:, cols],
+                in_=result_bf16[:, cols, :].rearrange("p j t -> p (j t)"),
             )
 
         def store_words(cols):
-            nc.sync.dma_start(out=word_rows[:, cols], in_=out_codes[:, cols].bitcast(I32))
+            nc.sync.dma_start(out=word_rows[:, cols], in_=result_codes[:, cols].bitcast(I32))
 
-        first, second, third = slice(0, 256), slice(256, 384), slice(384, 512)
-        low, high, every = slice(0, 2), slice(2, 4), slice(0, 4)
-        make_mixed(low, first)
-        make_mixed(high, first)
-        make_result(low, first)
-        make_result(high, first)
-        store_result(first)
-        round_result(first, False)
-        make_mixed(every, second)
-        make_mixed(every, third)
-        make_result(every, second)
-        store_result(second)
-        round_result(second, False)
-        quantize_result(first)
-        store_words(first)
-        make_result(every, third)
-        store_result(third)
-        quantize_result(second)
-        round_result(third, True)
-        quantize_result(third)
-        store_words(slice(256, 512))
-        for q in range(4):
+        first_half, second_half = slice(0, HALF), slice(HALF, S)
+        third_quarter, last_quarter = slice(HALF, S - P), slice(S - P, S)
+        pairs, all_slots = (slice(0, 2), slice(2, 4)), slice(0, PACK)
+        for slots in pairs:
+            make_mixed(slots, first_half)
+        for slots in pairs:
+            make_result(slots, first_half)
+        store_result(first_half)
+        round_result(first_half, False)
+        make_mixed(all_slots, third_quarter)
+        make_mixed(all_slots, last_quarter)
+        make_result(all_slots, third_quarter)
+        store_result(third_quarter)
+        round_result(third_quarter, False)
+        quantize_result(first_half)
+        store_words(first_half)
+        make_result(all_slots, last_quarter)
+        store_result(last_quarter)
+        quantize_result(third_quarter)
+        round_result(last_quarter, True)
+        quantize_result(last_quarter)
+        store_words(second_half)
+        for q in range(QUADRANTS):
             queue = nc.sync if q % 2 == 0 else nc.scalar
             queue.dma_start(
                 out=out_2[0, 4 * q : 4 * q + 4, :].bitcast(I32),
-                in_=out_plane[32 * q : 32 * q + 4, :].bitcast(I32),
+                in_=result_plane[32 * q : 32 * q + 4, :].bitcast(I32),
             )

from contextlib import ExitStack

import concourse.mybir as mybir
from concourse.masks import make_identity

K, T, S, N = 1024, 2048, 512, 512
FLOPS = 3 * 2 * K * N * S

F32 = mybir.dt.float32
BF16 = mybir.dt.bfloat16
I32 = mybir.dt.int32
U32 = mybir.dt.uint32
U16 = mybir.dt.uint16
U8 = mybir.dt.uint8
FP8X4 = mybir.dt.float8_e4m3fn_x4
ALU = mybir.AluOpType
SIGMOID = mybir.ActivationFunctionType.Sigmoid
TANH = mybir.ActivationFunctionType.Tanh
COPY = mybir.ActivationFunctionType.Copy

P = 128
PACK = 4
PASSES = K // (P * PACK)
QUADRANTS = P // 32
PAIRS = PACK // 2
HALF = S // 2
EARLY_SLOTS = 2


def tile_picked_sru8_none_po_kernel(
    tc, x_words, x_scales, cell, w1, w2, w3, hw, offs, par, out_0, out_1, out_2
):
    nc = tc.nc
    with ExitStack() as ctx:
        lists = ctx.enter_context(tc.tile_pool(name="lists", bufs=1))
        keep = ctx.enter_context(tc.tile_pool(name="keep", bufs=1))
        psum = ctx.enter_context(tc.psum_pool(name="psum", bufs=1))

        def slotted(name):
            return keep.tile([P, PACK, S], F32, name=name, align_bytes=64)

        def banks(name, tag):
            return [psum.tile([P, S], F32, name=f"{name}{t}", tag=f"{tag}{t}") for t in range(PACK)]

        offs_sb = lists.tile([P, S // 16], U16, name="offs_sb")
        par_sb = lists.tile([P, S // 16], U16, name="par_sb")
        word_table = [keep.tile([P, T], U32, name=f"word_table{g}", align_bytes=64) for g in range(PASSES)]
        scale_table = keep.tile([P, T], U8, name="scale_table", align_bytes=64)
        x_codes = [keep.tile([P, S], U32, name=f"x_codes{g}", align_bytes=64) for g in range(PASSES)]
        x_planes = keep.tile([P, S], U8, name="x_planes", align_bytes=64)
        cell_table = [keep.tile([P, S], F32, name=f"cell_table{t}", align_bytes=64) for t in range(PACK)]
        hw_sb = slotted("hw_sb")
        identity = keep.tile([P, P], F32, name="identity")

        weights = {"w1": w1, "w2": w2, "w3": w3}
        raw, rounded, codes, planes = {}, {}, {}, {}
        for name in weights:
            for g in range(PASSES):
                raw[name, g] = keep.tile([P, PACK, N], F32, name=f"raw_{name}_{g}", align_bytes=64)

        cell_rows = cell.rearrange("(p t) j -> p t j", t=PACK)
        hw_rows = hw.rearrange("(p t) j -> p t j", t=PACK)

        def load_weight(name, g):
            rows = weights[name][g * P * PACK : (g + 1) * P * PACK, :]
            nc.sync.dma_start(out=raw[name, g][:], in_=rows.rearrange("(p i) c -> p i c", i=PACK))

        def load_words(g):
            nc.sync.dma_start(
                out=word_table[g][:].bitcast(I32), in_=x_words[g].rearrange("p n i -> p (n i)").bitcast(I32)
            )

        def load_scales(g):
            for q in range(QUADRANTS):
                nc.sync.dma_start(
                    out=scale_table[32 * q + 4 * g : 32 * q + 4 * g + 4, :].bitcast(I32),
                    in_=x_scales[g, 4 * q : 4 * q + 4, :].bitcast(I32),
                )

        nc.vector.memset(scale_table[:].bitcast(I32), 0)
        make_identity(nc, identity[:])

        nc.sync.dma_start(par_sb[:], par)
        for t in range(EARLY_SLOTS):
            nc.sync.dma_start(out=cell_table[t][:], in_=cell_rows[:, t, :])
        load_weight("w2", 0)
        load_scales(0)
        nc.sync.dma_start(offs_sb[:], offs)
        load_words(0)
        load_scales(1)
        load_weight("w2", 1)
        load_words(1)
        for t in range(EARLY_SLOTS, PACK):
            nc.sync.dma_start(out=cell_table[t][:], in_=cell_rows[:, t, :])
        for name in ("w1", "w3"):
            for g in range(PASSES):
                load_weight(name, g)
        for h in range(PAIRS):
            nc.sync.dma_start(out=hw_sb[:, 2 * h : 2 * h + 2, :], in_=hw_rows[:, 2 * h : 2 * h + 2, :])

        def round_weight(name, g, h, on_vector):
            tag = f"rounded_{name}_{g}_{h}"
            rounded[name, g, h] = keep.tile([P, 2, P, PACK], BF16, name=tag, tag=tag, align_bytes=64)
            src = raw[name, g][:].rearrange("p i (m t) -> p m i t", t=PACK)[:, :, :, 2 * h : 2 * h + 2]
            dst = rounded[name, g, h][:].rearrange("p s m i -> p m i s")
            if name == "w1" and on_vector:
                nc.vector.tensor_scalar(out=dst, in0=src, scalar1=-1.0, scalar2=None, op0=ALU.mult)
            elif name == "w1":
                nc.scalar.activation(out=dst, in_=src, func=COPY, scale=-1.0)
            elif on_vector:
                nc.vector.tensor_copy(out=dst, in_=src)
            else:
                nc.scalar.copy(out=dst, in_=src)

        def quantize_weight(name, g, h, codes_tag):
            codes[name, g, h] = keep.tile([P, 2 * P], U32, name=f"codes_{name}_{g}_{h}", tag=codes_tag, align_bytes=64)
            planes[name, g, h] = keep.tile([P, 2 * P], U8, name=f"planes_{name}_{g}_{h}", align_bytes=64)
            nc.vector.quantize_mx(
                out=codes[name, g, h][:].bitcast(FP8X4),
                scales=planes[name, g, h][:],
                in_=rounded[name, g, h][:].rearrange("p s m i -> p (s m i)"),
            )

        def quantize(name, g, h):
            quantize_weight(name, g, h, f"codes_{name}_{g}_{h}")

        def multiply(name, g, t, bank):
            cols = slice((t % 2) * P, (t % 2 + 1) * P)
            nc.tensor.matmul_mx(
                out=bank[:],
                lhsT=codes[name, g, t // 2][:, cols].bitcast(FP8X4),
                lhsT_scale=planes[name, g, t // 2][:, cols],
                rhs=x_codes[g][:].bitcast(FP8X4),
                rhs_scale=x_planes[4 * g : P, :],
                start=(g == 0),
                stop=(g == PASSES - 1),
            )

        def turn(bank, row, first, last):
            for b in range(S // P):
                cols = slice(b * P, (b + 1) * P)
                nc.tensor.matmul(
                    out=bank[:, cols],
                    lhsT=row[:, cols],
                    rhs=identity[:],
                    is_transpose=True,
                    start=(first and b == 0),
                    stop=(last and b == S // P - 1),
                )

        c0 = slotted("c0")

        def gather_words(g):
            nc.vector.tensor_copy(out=x_codes[g][:], in_=word_table[g][:].indirect(offs_sb[:]))

        def gather_cell(t):
            for first in (0, HALF):
                nc.vector.tensor_copy(
                    out=c0[:, t, first : first + HALF],
                    in_=cell_table[t][:].indirect(par_sb[:, first // 16 : (first + HALF) // 16]),
                )

        fg = slotted("fg")
        z2 = banks("z2_", "gate")
        for t in range(EARLY_SLOTS):
            gather_cell(t)
        nc.vector.tensor_copy(out=x_planes[:], in_=scale_table[:].indirect(offs_sb[:]))
        for h in range(PAIRS):
            round_weight("w2", 0, h, False)
        gather_words(0)
        for h in range(PAIRS):
            quantize("w2", 0, h)
        for t in range(PACK):
            multiply("w2", 0, t, z2[t])
        for h in range(PAIRS):
            round_weight("w2", 1, h, h == 0)
        for h in range(PAIRS):
            quantize("w2", 1, h)
        gather_words(1)
        for t in range(PACK):
            multiply("w2", 1, t, z2[t])
            nc.scalar.activation(out=fg[:, t, :], in_=z2[t][:], func=SIGMOID)
        for t in range(EARLY_SLOTS, PACK):
            gather_cell(t)

        kept = slotted("kept")
        fresh = slotted("fresh")
        neg_y = banks("neg_y", "candidate")
        cn_turned = banks("cn_turned", "gate")
        for h in range(PAIRS):
            round_weight("w1", 0, h, False)
        quantize("w1", 0, 0)
        for t in (0, 1):
            multiply("w1", 0, t, neg_y[t])
        for h in range(PAIRS):
            round_weight("w1", 1, h, h == 0)
        quantize("w1", 1, 0)
        for t in (0, 1):
            multiply("w1", 1, t, neg_y[t])
        quantize_weight("w1", 0, 1, "rounded_w1_1_0")
        quantize("w1", 1, 1)
        for t in (2, 3):
            for g in range(PASSES):
                multiply("w1", g, t, neg_y[t])
        for t in range(PACK):
            nc.vector.tensor_tensor(out=kept[:, t, :], in0=c0[:, t, :], in1=fg[:, t, :], op=ALU.mult)
            turn(cn_turned[t], kept[:, t, :], True, False)
        for t in range(PACK):
            nc.vector.scalar_tensor_tensor(
                out=fresh[:, t, :], in0=fg[:, t, :], scalar=1.0, in1=neg_y[t][:], op0=ALU.subtract, op1=ALU.mult
            )
            turn(cn_turned[t], fresh[:, t, :], False, True)

        tanh_turned = slotted("tanh_turned")
        gap = slotted("gap")
        z3 = banks("z3_", "candidate")
        tanh_cn = banks("tanh_cn", "gate")

        def make_tanh(t):
            nc.scalar.activation(out=tanh_turned[:, t, :], in_=cn_turned[t][:], func=TANH)
            turn(tanh_cn[t], tanh_turned[:, t, :], True, True)

        def make_gap(t):
            nc.vector.tensor_tensor(out=gap[:, t, :], in0=tanh_cn[t][:], in1=hw_sb[:, t, :], op=ALU.subtract)

        for h in range(PAIRS):
            round_weight("w3", 0, h, False)
        for t in (0, 1):
            make_tanh(t)
        for h in range(PAIRS):
            quantize("w3", 0, h)
        for t in range(PACK):
            multiply("w3", 0, t, z3[t])
        for h in range(PAIRS):
            round_weight("w3", 1, h, h == 0)
        for t in (2, 3):
            make_tanh(t)
        for h in range(PAIRS):
            quantize("w3", 1, h)
            for t in (2 * h, 2 * h + 1):
                multiply("w3", 1, t, z3[t])
            for t in (2 * h, 2 * h + 1):
                make_gap(t)

        rg = slotted("rg")
        mixed = slotted("mixed")
        result = slotted("result")
        result_bf16 = keep.tile([P, S, PACK], BF16, name="result_bf16", align_bytes=64)
        result_codes = keep.tile([P, S], U32, name="result_codes", align_bytes=64)
        result_plane = keep.tile([P, S], U8, name="result_plane", align_bytes=64)
        out_rows = out_0.rearrange("(p t) j -> p t j", t=PACK)
        word_rows = out_1[0].rearrange("p n i -> p (n i)").bitcast(I32)

        for first in (0, HALF):
            for t in range(PACK):
                cols = slice(first, first + HALF)
                nc.scalar.activation(out=rg[:, t, cols], in_=z3[t][:, cols], func=SIGMOID)

        def make_mixed(slots, cols):
            nc.vector.tensor_tensor(
                out=mixed[:, slots, cols], in0=gap[:, slots, cols], in1=rg[:, slots, cols], op=ALU.mult
            )

        def make_result(slots, cols):
            nc.vector.tensor_tensor(
                out=result[:, slots, cols], in0=mixed[:, slots, cols], in1=hw_sb[:, slots, cols], op=ALU.add
            )

        def store_result(cols):
            nc.sync.dma_start(out=out_rows[:, :, cols], in_=result[:, :, cols])

        def round_result(cols, on_vector):
            dst = result_bf16[:, cols, :].rearrange("p (c i) t -> p c t i", i=4)
            src = result[:, :, cols].rearrange("p t (c i) -> p c t i", i=4)
            if on_vector:
                nc.vector.tensor_copy(out=dst, in_=src)
            else:
                nc.scalar.copy(out=dst, in_=src)

        def quantize_result(cols):
            nc.vector.quantize_mx(
                out=result_codes[:, cols].bitcast(FP8X4),
                scales=result_plane[:, cols],
                in_=result_bf16[:, cols, :].rearrange("p j t -> p (j t)"),
            )

        def store_words(cols):
            nc.sync.dma_start(out=word_rows[:, cols], in_=result_codes[:, cols].bitcast(I32))

        first_half, second_half = slice(0, HALF), slice(HALF, S)
        third_quarter, last_quarter = slice(HALF, S - P), slice(S - P, S)
        pairs, all_slots = (slice(0, 2), slice(2, 4)), slice(0, PACK)
        for slots in pairs:
            make_mixed(slots, first_half)
        for slots in pairs:
            make_result(slots, first_half)
        store_result(first_half)
        round_result(first_half, False)
        make_mixed(all_slots, third_quarter)
        make_mixed(all_slots, last_quarter)
        make_result(all_slots, third_quarter)
        store_result(third_quarter)
        round_result(third_quarter, False)
        quantize_result(first_half)
        store_words(first_half)
        make_result(all_slots, last_quarter)
        store_result(last_quarter)
        quantize_result(third_quarter)
        round_result(last_quarter, True)
        quantize_result(last_quarter)
        store_words(second_half)
        for q in range(QUADRANTS):
            queue = nc.sync if q % 2 == 0 else nc.scalar
            queue.dma_start(
                out=out_2[0, 4 * q : 4 * q + 4, :].bitcast(I32),
                in_=result_plane[32 * q : 32 * q + 4, :].bitcast(I32),
            )
